import numpy as np
CORES = [31,71,111]
N = 3
C, TIMES = 512, 2
def setup_inputs(rng):
    return {"x": np.exp(rng.standard_normal((N, 128, C), dtype=np.float32))}
def setup_inputs_big(rng):
    d = setup_inputs(rng)
    for k in ("x",): d[k] = (d[k].astype(np.float32) * 1048576.0).astype(d[k].dtype)
    return d
def setup_inputs_small(rng):
    d = setup_inputs(rng)
    for k in ("x",): d[k] = (d[k].astype(np.float32) * (1 / 1048576.0)).astype(d[k].dtype)
    return d
def setup_inputs_mixed(rng):
    d = setup_inputs(rng)
    f = (10.0 ** rng.uniform(-3, 3, (1, 1, C))).astype(np.float32)
    for k in ("x",): d[k] = (d[k].astype(np.float32) * f).astype(d[k].dtype)
    return d
def reference(x):
    X = x.astype(np.float64)
    for _ in range(TIMES):
        X = X / X.sum(axis=2, keepdims=True)
        X = X / X.sum(axis=(0, 1), keepdims=True)
    return {"y": X.astype(np.float32)}

from concourse.bass import DstId, RemoteDMATransfer
from concourse.mybir import AluOpType, AxisListType, ActivationFunctionType

NR = 3
P = 128
C = 512
NB = C // P
PIECES = [(0, 64), (64, 64), (128, 128), (256, 128), (384, 64), (448, 64)]
HALF = C // 2

SCRATCH = {
    "x0": ("sbuf", [P, C], "float32"),
    "xt": ("sbuf", [P, C], "float32"),
    "ones": ("sbuf", [P, P], "float32"),
    "ident": ("sbuf", [P, P], "float32"),
    "junk": ("sbuf", [P, C // 2], "float32"),
    "rs": ("sbuf", [P, 2], "float32"),
    "rsum": ("sbuf", [P, 1], "float32"),
    "r1": ("sbuf", [P, 1], "float32"),
    "rr": ("sbuf", [P, 1], "float32"),
    "p1": ("sbuf", [P, NB], "float32"),
    "p2": ("sbuf", [P, NB], "float32"),
    "land1": ("sbuf", [P, NB * NR], "float32"),
    "land2": ("sbuf", [P, NB * NR], "float32"),
    "h1": ("sbuf", [P, NB], "float32"),
    "h2": ("sbuf", [P, NB], "float32"),
    "s1": ("sbuf", [P, NB], "float32"),
    "s2": ("sbuf", [P, NB], "float32"),
    "c1": ("sbuf", [P, NB], "float32"),
    "c2": ("sbuf", [P, NB], "float32"),
    "dg": ("sbuf", [P, C], "float32"),
    "yb": ("sbuf", [P, C], "float32"),
    "b0": ("psum", [P, C], "float32"),
    "b1": ("psum", [P, C], "float32"),
    "b2": ("psum", [P, C], "float32"),
    "b3": ("psum", [P, C], "float32"),
    "b4": ("psum", [P, C], "float32"),
    "b5": ("psum", [P, C], "float32"),
    "b6": ("psum", [P, C], "float32"),
}
SEMAPHORES = (["ld", "ones", "ident", "rs", "rsum", "r1", "mm1", "p1", "xt", "h1", "s1", "c1", "mmt", "rr", "mmu", "p2",
               "h2", "s2", "c2", "sent", "st", "e0", "e1"]
              + ["t%d" % k for k in range(NB)]
              + ["a1_%d" % q for q in range(NR)] + ["a2_%d" % q for q in range(NR)]
              + ["d%d" % i for i in range(len(PIECES))] + ["f%d" % i for i in range(len(PIECES))])


def rank_program(g, core, T, topo):
    rank = T.rank_of(core)
    if rank is None:
        return
    S = T.sem
    cores = list(T.cores)
    v, act, pe, sy = g.vector, g.scalar, g.tensor, g.sync
    ADD, MUL = AluOpType.add, AluOpType.mult
    COPY = ActivationFunctionType.Copy

    def blk(t, k):
        return t[:, P * k:P * (k + 1)]

    def hops(a, b):
        ca, cb = topo.chip(a), topo.chip(b)
        if ca == cb:
            return 0
        return 1 if (topo.mates(ca, cb) or topo.same_plane(ca, cb)) else 2

    def send_order(r):
        return sorted([q for q in range(len(cores)) if q != r], key=lambda q: (-hops(cores[r], cores[q]), q))

    dsts = send_order(rank)
    recv = sorted(dsts, key=lambda q: (send_order(q).index(rank), hops(cores[q], core), q))
    mask = topo.mask(core, cores[dsts[0]])
    for q in dsts:
        if not topo.may_write(core, cores[q]):
            raise ValueError("rank %d may not write to rank %d directly" % (rank, q))
        mask &= topo.mask(core, cores[q])
    engines = bin(mask).count("1")
    ids = []
    for q in dsts:
        rid, pid, _se = topo.addr(cores[q])
        ids.append(DstId(rid=rid, pnc=pid))

    def send(src, land, sem):
        slot = land[:, NB * rank:NB * (rank + 1)]
        g.remote_dma_fused([RemoteDMATransfer(dst_ids=ids, dma_engine_mask=mask, remote_sem=sem, srcs=[src[:, :]],
                                              dsts=[slot for _q in ids], alu_op=0)], local_sem=S.sent)

    def gather(own, own_sem, land, arr, h, h_sem, s, s_sem, c, c_sem):
        q0, q1 = recv
        v.wait_ge(own_sem, 1)
        v.wait_ge(S[arr % q0], engines)
        v.tensor_tensor(h[:, :], own[:, :], land[:, NB * q0:NB * (q0 + 1)], ADD).then_inc(h_sem, 1)
        v.wait_ge(S[arr % q1], engines)
        v.wait_ge(h_sem, 1)
        v.tensor_tensor(s[:, :], h[:, :], land[:, NB * q1:NB * (q1 + 1)], ADD).then_inc(s_sem, 1)
        v.wait_ge(s_sem, 1)
        v.reciprocal(c[:, :], s[:, :]).then_inc(c_sem, 1)

    sy.dma_start(T.x0[:, :], T.x[:, :]).then_inc(S.ld, 16)
    v.memset(T.ones[:, :], 1.0).then_inc(S.ones, 1)
    g.wait_ge(S.ones, 1)
    g.affine_select(T.ident[:, :], T.ones[:, :], [[-1, P]], AluOpType.is_equal, 0.0, 0, 1).then_inc(S.ident, 1)

    v.wait_ge(S.ld, 16)
    v.tensor_reduce(T.rs[:, 0:1], T.x0[:, 0:HALF], AxisListType.X, ADD).then_inc(S.rs, 1)
    act.wait_ge(S.ld, 16)
    act.activation(T.junk[:, :], T.x0[:, HALF:C], COPY, accum_out=T.rs[:, 1:2]).then_inc(S.rs, 1)
    v.wait_ge(S.rs, 2)
    v.tensor_tensor(T.rsum[:, :], T.rs[:, 0:1], T.rs[:, 1:2], ADD).then_inc(S.rsum, 1)
    v.wait_ge(S.rsum, 1)
    v.reciprocal(T.r1[:, :], T.rsum[:, :]).then_inc(S.r1, 1)

    tb = [T.b0, T.b1, T.b2, T.b3]

    def transpose(k):
        pe.matmul(tb[k][:, 0:P], blk(T.x0, k), T.ident[:, :], True, True).then_inc(S["t%d" % k], 1)

    pe.wait_ge(S.ld, 16)
    pe.wait_ge(S.ident, 1)
    transpose(0)
    pe.wait_ge(S.r1, 1)
    for k in range(NB):
        pe.matmul(T.b4[:, k:k + 1], blk(T.x0, k), T.r1[:, :], True, True).then_inc(S.mm1, 1)
    for k in range(1, NB):
        transpose(k)
    for k in range(NB):
        act.wait_ge(S["t%d" % k], 1)
        act.activation(blk(T.xt, k), tb[k][:, 0:P], COPY).then_inc(S.xt, 1)

    v.wait_ge(S.mm1, NB)
    v.tensor_copy(T.p1[:, :], T.b4[:, 0:NB]).then_inc(S.p1, 1)
    g.wait_ge(S.p1, 1)
    send(T.p1, T.land1, S["a1_%d" % rank])
    gather(T.p1, S.p1, T.land1, "a1_%d", T.h1, S.h1, T.s1, S.s1, T.c1, S.c1)

    pe.wait_ge(S.xt, NB)
    pe.wait_ge(S.c1, 1)
    for k in range(NB):
        pe.matmul(T.b5[:, 0:1], blk(T.xt, k), T.c1[:, k:k + 1], k == 0, k == NB - 1).then_inc(S.mmt, 1)
    v.wait_ge(S.mmt, NB)
    v.reciprocal(T.rr[:, :], T.b5[:, 0:1]).then_inc(S.rr, 1)
    pe.wait_ge(S.rr, 1)
    for k in range(NB):
        pe.matmul(T.b6[:, k:k + 1], blk(T.x0, k), T.rr[:, :], True, True).then_inc(S.mmu, 1)

    v.wait_ge(S.mmu, NB)
    v.tensor_copy(T.p2[:, :], T.b6[:, 0:NB]).then_inc(S.p2, 1)
    g.wait_ge(S.p2, 1)
    send(T.p2, T.land2, S["a2_%d" % rank])
    gather(T.p2, S.p2, T.land2, "a2_%d", T.h2, S.h2, T.s2, S.s2, T.c2, S.c2)

    fb = [T.b0, T.b1, T.b2, T.b3, T.b4, T.b5]
    v.wait_ge(S.c2, 1)
    v.wait_ge(S.rr, 1)
    act.wait_ge(S.c2, 1)
    act.wait_ge(S.rr, 1)
    for i, (c0, w) in enumerate(PIECES):
        k, o = c0 // P, c0 % P
        if i % 2 == 0:
            v.tensor_scalar(T.dg[:, c0:c0 + w], T.ident[:, o:o + w], T.c2[:, k:k + 1], None, MUL).then_inc(S["d%d" % i], 1)
        else:
            act.activation(T.dg[:, c0:c0 + w], T.ident[:, o:o + w], COPY, scale=T.c2[:, k:k + 1]).then_inc(S["d%d" % i], 1)
    for i, (c0, w) in enumerate(PIECES):
        pe.wait_ge(S["d%d" % i], 1)
        pe.matmul(fb[i][:, 0:w], blk(T.xt, c0 // P), T.dg[:, c0:c0 + w], True, True).then_inc(S["f%d" % i], 1)
    count = [0, 0]
    for i, (c0, w) in enumerate(PIECES):
        e = c0 // HALF
        count[e] += 1
        if i % 2 == 0:
            v.wait_ge(S["f%d" % i], 1)
            v.tensor_scalar(T.yb[:, c0:c0 + w], fb[i][:, 0:w], T.rr[:, 0:1], None, MUL).then_inc(S["e%d" % e], 1)
        else:
            act.wait_ge(S["f%d" % i], 1)
            act.activation(T.yb[:, c0:c0 + w], fb[i][:, 0:w], COPY, scale=T.rr[:, 0:1]).then_inc(S["e%d" % e], 1)

    for e in range(2):
        sy.wait_ge(S["e%d" % e], count[e])
        sy.dma_start(T.y[:, HALF * e:HALF * (e + 1)], T.yb[:, HALF * e:HALF * (e + 1)]).then_inc(S.st, 16)
    sy.wait_ge(S.st, 32)
    g.wait_ge(S.sent, 2 * engines)
